import numpy as np
import ml_dtypes


def mxq(x, axis, fmt="e4m3"):
    dtype, down = {"e4m3": (ml_dtypes.float8_e4m3fn, 7), "e5m2": (ml_dtypes.float8_e5m2, 14)}[fmt]
    v = np.moveaxis(np.asarray(x, np.float32).astype(ml_dtypes.bfloat16).astype(np.float64), axis, -1)
    blocks = v.reshape(v.shape[:-1] + (-1, 32))
    amax = np.abs(blocks).max(-1, keepdims=True)
    byte = np.maximum(np.where(amax > 0, np.frexp(amax)[1] - 1 + 127, 0) - down, 1)
    scale = np.exp2(byte - 127.0)
    codes = (blocks / scale).astype(np.float32).astype(dtype).astype(np.float64)
    return np.moveaxis((codes * scale).reshape(v.shape), -1, axis)


WIDE = False


def mx_kscale(k):
    if not WIDE:
        return np.ones(k)
    levels = np.array([10, -10, 5, -5, 0])
    if k % 512:
        return np.exp2(np.random.permutation(np.resize(levels, k // 32))).repeat(32)
    a = np.empty((k // 512, 16))
    for p in range(k // 512):
        a[p, :8] = np.random.permutation(np.resize(levels, 8))
        for g in range(8):
            far = levels[np.abs(levels - a[p, g]) >= 10]
            a[p, g + 8] = far[np.random.randint(len(far))]
    return np.exp2(a.ravel()).repeat(32)


BF16 = ml_dtypes.bfloat16


def bf(x):
    return np.asarray(x, np.float32).astype(BF16)


def f64(x):
    return np.asarray(x).astype(np.float64)


L, P, B, D, T = 3, 2, 4096, 512, 512


def scaled_message(n):
    w = np.exp(n - n.max(-1, keepdims=True))
    return n.shape[-1] * (w / w.sum(-1, keepdims=True))


def log_normalise(q):
    top = q.max(-1, keepdims=True)
    log_z = top + np.log(np.sum(np.exp(q - top), axis=-1, keepdims=True))
    return q - log_z + np.log(q.shape[-1])


def draw0():
    s = mx_kscale(D)
    t = np.stack([mx_kscale(T) for _ in range(P)])
    return {
        "x": bf(np.random.standard_normal((L, B, D)) * s),
        "we": bf(np.random.standard_normal((D, T)) / np.sqrt(D) / s[:, None]),
        "be": bf(0.3 * np.random.standard_normal(T)),
        "ends": bf(0.5 * np.random.standard_normal((P, T))),
        "gain": bf(np.random.standard_normal((P, T)) * t),
        "trans": bf(np.random.standard_normal((P, T, T)) * 3.5 / np.sqrt(T) / t[:, :, None]),
    }


def core(x, we, be, ends, gain, trans):
    e = (mxq(f64(x), 2, "e4m3") @ mxq(f64(we), 0, "e4m3")) + f64(be)
    en = f64(ends)
    n = np.stack([e[0] + en[0], e[2] + en[1]], axis=0)
    u = scaled_message(n)
    v = u * f64(gain)[:, None, :]
    m = mxq(v, 2, "e4m3") @ mxq(f64(trans), 1, "e4m3")
    c = np.log(np.maximum(1.0 + m / 16.0, 0.1))
    q = e[1] + c[0] + c[1]
    return log_normalise(q)


def e4m3fn_bytes(y):
    return np.clip(np.asarray(y, np.float64), -448.0, 448.0).astype(np.float32).astype(ml_dtypes.float8_e4m3fn).view(np.uint8)


def e4m3fn_values(b):
    return np.asarray(b, np.uint8).view(ml_dtypes.float8_e4m3fn).astype(np.float64)


def setup_inputs():
    d = draw0()
    x0 = np.asarray(d['x']).astype(np.float64)
    s = (np.max(np.abs(x0), axis=(0, 1), keepdims=True) / 448.0).astype(np.float32)
    out = {}
    for k, v in d.items():
        if k == 'x':
            out['x_bytes'] = e4m3fn_bytes(x0 / s.astype(np.float64))
            out['x_scale'] = s
        else:
            out[k] = v
    return out


def reference(x_bytes, x_scale, we, be, ends, gain, trans):
    return core(e4m3fn_values(x_bytes) * x_scale.astype(np.float64), we, be, ends, gain, trans)

@@ -1,0 +1,471 @@
+from contextlib import ExitStack
+
+import concourse.mybir as mybir
+from concourse.masks import make_identity
+
+L, NB, B, D, T = 3, 2, 4096, 512, 512
+FLOPS = 2 * (L + NB) * B * D * T
+
+F32 = mybir.dt.float32
+BF16 = mybir.dt.bfloat16
+U32 = mybir.dt.uint32
+U8 = mybir.dt.uint8
+FP8 = mybir.dt.float8_e4m3fn
+FP8X4 = mybir.dt.float8_e4m3fn_x4
+ALU = mybir.AluOpType
+ACT = mybir.ActivationFunctionType
+AXIS = mybir.AxisListType
+
+P = 128
+PACK = 4
+QUAD = 512
+TILES = QUAD // P
+QUADS = B // QUAD
+CHUNKS = T // P
+UNITS = NB * TILES
+BANKS = 8
+GROUPS = (3, 3, 2)
+VECTOR_CLAMPS = 4
+VECTOR_EXITS = 1
+GAP = 2
+LOG_LEAD = 2
+X_DELAY = 8
+BE_ROW = 32
+NEIGHBOUR_OF = (0, 2)
+MIDDLE = 1
+
+
+def tile_chunkflooredmessagemiddlescore_t_kernel(tc, x_bytes, x_scale, we, be, ends, gain, trans, out):
+    nc = tc.nc
+    with ExitStack() as ctx:
+        sb = ctx.enter_context(tc.tile_pool(name="sb", bufs=1))
+        ps = ctx.enter_context(tc.psum_pool(name="ps", bufs=1))
+        ctx.enter_context(tc.manual_schedule())
+
+        group_max = max(GROUPS)
+        free_banks = list(range(BANKS))
+        held = {}
+
+        def take_bank(dtype=F32, width=T):
+            index = free_banks[0]
+            free_banks.remove(index)
+            bank = ps.tile([P, width], dtype, tag="bank%d" % index, name="bank%d" % index)
+            return bank, index
+
+        def new_tile(tag, shape, dtype, bufs):
+            return sb.tile(shape, dtype, tag=tag, name=tag, bufs=bufs, align_bytes=64)
+
+        def interleaved_tile():
+            return new_tile("interleaved", [P, QUAD * PACK], BF16, 4)
+
+        def score_tile():
+            return new_tile("scores", [P, TILES, T], F32, group_max + 2)
+
+        def quantise(source, tag, bufs):
+            codes = new_tile(tag + "_codes", [P, QUAD], U32, bufs)
+            scales = new_tile(tag + "_scales", [P, QUAD], U8, bufs)
+            nc.vector.quantize_mx(out=codes[:].bitcast(FP8X4), scales=scales[:], in_=source[:])
+            return codes, scales
+
+        def product(weights, c, moving):
+            bank, index = take_bank()
+            cols = slice(c * P, (c + 1) * P)
+            nc.tensor.matmul_mx(
+                out=bank[:], lhsT=weights[0][:, cols].bitcast(FP8X4), lhsT_scale=weights[1][:, cols],
+                rhs=moving[0][:].bitcast(FP8X4), rhs_scale=moving[1][:], start=True, stop=True)
+            return bank, index
+
+        ident = new_tile("ident", [P, P], F32, 1)
+        ident_half = new_tile("ident_half", [P, P], BF16, 1)
+        scale_rows = new_tile("scale_rows", [P, 2, D], F32, 1)
+        gain_rows = new_tile("gain_rows", [P, NB, T], F32, 1)
+        bias_cols = new_tile("bias_cols", [P, CHUNKS, P], F32, 1)
+        offsets = new_tile("offsets", [P, 3], F32, 1)
+
+        def load_bytes(q, l):
+            raw = new_tile("x_raw", [P, TILES * D], U8, 4)
+            rows = x_bytes[l, q * QUAD:(q + 1) * QUAD, :]
+            nc.sync.dma_start(out=raw[:], in_=rows.rearrange("(p j) k -> p (j k)", j=TILES))
+            held["raw", q, l] = raw
+
+        def load_constants():
+            scale_cols = new_tile("scale_cols", [P, PACK], F32, 1)
+            nc.sync.dma_start(out=scale_cols[:], in_=x_scale.rearrange("a b (p t) -> p (a b t)", t=PACK))
+            held["scale_cols"] = scale_cols
+            load_bytes(0, NEIGHBOUR_OF[0])
+            we_raw = score_tile()
+            we_view = we_raw[:].rearrange("p j t -> p (j t)").bitcast(BF16)[:, 0:PACK * T]
+            nc.sync.dma_start(out=we_view, in_=we.rearrange("(p j) n -> p (j n)", j=PACK))
+            held["we_raw"] = we_view
+            be_rows = new_tile("be_rows", [P, T], BF16, 1)
+            end_rows = new_tile("end_rows", [P, T], BF16, 1)
+            nc.sync.dma_start(out=be_rows[0:NB, :], in_=be.partition_broadcast(NB))
+            nc.sync.dma_start(out=end_rows[0:NB, :], in_=ends)
+            nc.sync.dma_start(out=be_rows[BE_ROW:BE_ROW + 1, :], in_=be.rearrange("(o t) -> o t", o=1))
+            held["be_rows"] = be_rows
+            held["end_rows"] = end_rows
+            load_bytes(0, NEIGHBOUR_OF[1])
+            load_bytes(0, MIDDLE)
+
+        def load_late_constants():
+            gain_raw = new_tile("gain_raw", [P, NB, PACK], BF16, 1)
+            nc.sync.dma_start(out=gain_raw[:], in_=gain.rearrange("n (p t) -> p n t", t=PACK))
+            held["gain_raw"] = gain_raw
+            trans_raw = score_tile()
+            trans_view = trans_raw[:].rearrange("p j t -> p (j t)").bitcast(BF16).rearrange("p (n r) -> p n r", n=NB)
+            nc.sync.dma_start(out=trans_view, in_=trans.rearrange("n (p j) t -> p n (j t)", j=PACK))
+            held["trans_raw"] = trans_view
+
+        def make_constants():
+            make_identity(nc, ident[:])
+            make_identity(nc, ident_half[:])
+            bias_rows = new_tile("weights", [P, T], F32, 4)
+            nc.gpsimd.memset(bias_rows[:], 0.0)
+            nc.gpsimd.memset(offsets[:, 0:1], 9.0)
+            nc.gpsimd.memset(offsets[:, 1:2], 1.0)
+            nc.gpsimd.memset(offsets[:, 2:3], 10.0)
+            held["bias_rows"] = bias_rows
+
+        def spread(cols):
+            bank, index = take_bank()
+            for t in range(PACK):
+                nc.tensor.transpose(bank[:, t * P:(t + 1) * P], cols[:, t:t + 1].to_broadcast([P, P]), ident[:])
+            return bank, index
+
+        def make_scales():
+            bank, index = spread(held["scale_cols"])
+            nc.scalar.copy(out=scale_rows[:, 0, :].rearrange("r (p t) -> r p t", t=PACK), in_=bank[:].rearrange("r (t p) -> r p t", t=PACK))
+            nc.scalar.copy(out=scale_rows[:, 1, :], in_=scale_rows[:, 0, :])
+            free_banks.append(index)
+
+        def make_biases():
+            bias_rows = held["bias_rows"]
+            nc.vector.tensor_tensor(
+                out=bias_rows[0:NB, :].rearrange("r (u p e) -> r u p e", u=2, e=2),
+                in0=held["be_rows"][0:NB, :].rearrange("r (p u e) -> r u p e", u=2, e=2),
+                in1=held["end_rows"][0:NB, :].rearrange("r (p u e) -> r u p e", u=2, e=2), op=ALU.add)
+            nc.vector.tensor_copy(out=bias_rows[BE_ROW:BE_ROW + 1, :], in_=held["be_rows"][BE_ROW:BE_ROW + 1, :])
+            bank, index = take_bank()
+            for c in range(CHUNKS):
+                nc.tensor.transpose(bank[:, c * P:(c + 1) * P], bias_rows[:, c * P:(c + 1) * P], ident[:])
+            nc.scalar.copy(out=bias_cols[:].rearrange("p c r -> p (c r)"), in_=bank[:])
+            free_banks.append(index)
+
+        def make_gains(n):
+            gain_cols = new_tile("gain_cols", [P, PACK], F32, NB)
+            nc.vector.tensor_scalar(out=gain_cols[:], in0=held["gain_raw"][:, n, :], scalar1=float(T), scalar2=None, op0=ALU.mult)
+            bank, index = spread(gain_cols)
+            nc.scalar.copy(out=gain_rows[:, n, :].rearrange("r (u p e) -> r u p e", u=2, e=2),
+                           in_=bank[:].rearrange("r (u e p) -> r u p e", u=2, e=2))
+            free_banks.append(index)
+
+        def interleave_we_permuted():
+            grouped = interleaved_tile()
+            nc.scalar.copy(
+                out=grouped[:].rearrange("r (u p e j) -> r u p e j", u=2, e=2, j=PACK),
+                in_=held["we_raw"].rearrange("r (j p u e) -> r u p e j", j=PACK, u=2, e=2))
+            held["grouped", "we_nb"] = grouped
+
+        def interleave_natural(key, raw):
+            grouped = interleaved_tile()
+            nc.scalar.copy(out=grouped[:].rearrange("r (n j) -> r n j", j=PACK), in_=raw.rearrange("r (j n) -> r n j", j=PACK))
+            held["grouped", key] = grouped
+
+        def interleave_we():
+            interleave_natural("we_mid", held["we_raw"])
+
+        def interleave_trans(n):
+            interleave_natural(("trans", n), held["trans_raw"][:, n, :])
+
+        def quantise_weights(key):
+            held["weights", key] = quantise(held["grouped", key], "w", 2 + NB)
+
+        def scale_x(q, l, h):
+            scaled = new_tile("scaled", [P, 2 * D], BF16, 3)
+            nc.vector.tensor_tensor(
+                out=scaled[:], in0=held["raw", q, l][:, h * 2 * D:(h + 1) * 2 * D].bitcast(FP8),
+                in1=scale_rows[:].rearrange("p j k -> p (j k)"), op=ALU.mult)
+            held["scaled", q, l, h] = scaled
+
+        def turn_x(q, l, h):
+            words = held["scaled", q, l, h][:].bitcast(F32)
+            bank, index = take_bank()
+            for j in range(2):
+                for u in range(2):
+                    nc.tensor.transpose(
+                        bank[:, (2 * j + u) * P:(2 * j + u + 1) * P],
+                        words[:, j * 2 * P + u:(j + 1) * 2 * P:2], ident[:])
+            held["x_bank", q, l, h] = (bank, index)
+
+        def empty_words(bank_key, grouped_key, h):
+            if h == 0:
+                held[grouped_key] = interleaved_tile()
+            bank, index = held[bank_key]
+            words = held[grouped_key][:].bitcast(F32)[:, h * T:(h + 1) * T]
+            nc.scalar.copy(
+                out=words.rearrange("p (j r u) -> p j r u", j=2, u=2),
+                in_=bank[:].rearrange("p (j u r) -> p j r u", j=2, u=2))
+            free_banks.append(index)
+
+        def empty_x(q, l, h):
+            empty_words(("x_bank", q, l, h), ("x_grouped", q, l), h)
+
+        def quantise_x(q, l):
+            if l == MIDDLE:
+                held["x", q, l] = quantise(held["x_grouped", q, l], "x_mid", group_max + 2)
+            else:
+                held["x", q, l] = quantise(held["x_grouped", q, l], "x_nb", 2)
+
+        def multiply_neighbour(q, n, c):
+            held["e_bank", q, n, c] = product(held["weights", "we_nb"], c, held["x", q, NEIGHBOUR_OF[n]])
+
+        def empty_neighbour(q, n, c):
+            if c == 0:
+                held["n_t", q, n] = new_tile("n_t", [P, CHUNKS, QUAD], F32, 4)
+            bank, index = held["e_bank", q, n, c]
+            if n * CHUNKS + c < VECTOR_EXITS:
+                nc.vector.tensor_scalar(out=held["n_t", q, n][:, c, :], in0=bank[:], scalar1=bias_cols[:, c, n:n + 1], scalar2=None, op0=ALU.add)
+            else:
+                nc.scalar.activation(out=held["n_t", q, n][:, c, :], in_=bank[:], func=ACT.Identity, bias=bias_cols[:, c, n:n + 1])
+            free_banks.append(index)
+
+        def turn_neighbour(q, n, j):
+            bank, index = take_bank()
+            for c in range(CHUNKS):
+                nc.tensor.transpose(bank[:, c * P:(c + 1) * P], held["n_t", q, n][:, c, j * P:(j + 1) * P], ident[:])
+            held["n_bank", q, n, j] = (bank, index)
+
+        def turn_upper_halves(q, n, h):
+            bank, index = take_bank(BF16, 2 * T)
+            for i in range(2):
+                j = 2 * h + i
+                for c in range(CHUNKS):
+                    halves = held["n_t", q, n][:, c, :].bitcast(BF16)
+                    nc.tensor.transpose(bank[:, i * T + c * P:i * T + (c + 1) * P],
+                                        halves[:, 2 * j * P + 1:2 * (j + 1) * P:2], ident_half[:])
+            held["top_bank", q, n, h] = (bank, index)
+
+        def neighbour_max(q, n, j):
+            if j == 0:
+                held["neg_max", q, n] = new_tile("neg_max", [P, TILES], F32, 3)
+            bank, index = held["top_bank", q, n, j // 2]
+            negated = new_tile("negated", [P, T], BF16, 1)
+            nc.vector.tensor_scalar(out=negated[:], in0=bank[:, (j % 2) * T:(j % 2 + 1) * T], scalar1=-1.0, scalar2=None,
+                                    op0=ALU.mult, op1=ALU.min, accum_out=held["neg_max", q, n][:, j:j + 1])
+            if j % 2 == 1:
+                free_banks.append(index)
+
+        def neighbour_exp(q, n, j):
+            if j == 0:
+                held["sums", q, n] = new_tile("sums", [P, TILES], F32, 3)
+            bank, index = held["n_bank", q, n, j]
+            w = new_tile("weights", [P, T], F32, 4)
+            nc.scalar.activation(out=w[:], in_=bank[:], func=ACT.Exp, bias=held["neg_max", q, n][:, j:j + 1],
+                                 accum_out=held["sums", q, n][:, j:j + 1])
+            free_banks.append(index)
+            held["w", q, n, j] = w
+
+        def reciprocals(q, n, h):
+            if h == 0:
+                held["recip", q, n] = new_tile("recip", [P, TILES], F32, 3)
+            nc.vector.reciprocal(out=held["recip", q, n][:, 2 * h:2 * h + 2], in_=held["sums", q, n][:, 2 * h:2 * h + 2])
+
+        def apply_gain(q, n, j):
+            if j % 2 == 0:
+                held["v", q, n, j // 2] = new_tile("v", [P, 2, T], BF16, 2)
+            nc.vector.scalar_tensor_tensor(
+                out=held["v", q, n, j // 2][:, j % 2, :], in0=held["w", q, n, j][:], scalar=held["recip", q, n][:, j:j + 1],
+                in1=gain_rows[:, n, :], op0=ALU.mult, op1=ALU.mult)
+
+        def turn_v(q, n, h):
+            words = held["v", q, n, h][:].rearrange("p j t -> p (j t)").bitcast(F32)
+            bank, index = take_bank()
+            for i in range(4):
+                nc.tensor.transpose(bank[:, i * P:(i + 1) * P], words[:, i * P:(i + 1) * P], ident[:])
+            held["v_bank", q, n, h] = (bank, index)
+
+        def empty_v(q, n, h):
+            empty_words(("v_bank", q, n, h), ("v_grouped", q, n), h)
+
+        def quantise_v(q, n):
+            held["v_codes", q, n] = quantise(held["v_grouped", q, n], "v", NB * group_max + 1)
+
+        def multiply_message(q, n, c):
+            held["m_bank", q, n, c] = product(held["weights", ("trans", n)], c, held["v_codes", q, n])
+
+        def clamp(q, n, c):
+            bank, index = held["m_bank", q, n, c]
+            floored = new_tile("floored", [P, QUAD], F32, 4)
+            if n * CHUNKS + c < VECTOR_CLAMPS:
+                nc.vector.tensor_scalar(out=floored[:], in0=bank[:], scalar1=0.625, scalar2=-9.0, op0=ALU.mult, op1=ALU.max)
+                held["floored", q, n, c] = (floored, offsets[:, 2:3])
+            else:
+                nc.scalar.activation(out=floored[:], in_=bank[:], func=ACT.Relu, scale=0.625, bias=offsets[:, 0:1])
+                held["floored", q, n, c] = (floored, offsets[:, 1:2])
+            free_banks.append(index)
+
+        def log_message(q, n, c):
+            floored, offset = held["floored", q, n, c]
+            if n == 0:
+                logs = new_tile("log_first", [P, QUAD], F32, 3)
+            else:
+                logs = new_tile("log_second", [P, QUAD], F32, 2 * CHUNKS)
+            nc.scalar.activation(out=logs[:], in_=floored[:], func=ACT.Ln, bias=offset)
+            held["log", q, n, c] = logs
+
+        def multiply_middle(q, c):
+            held["mid_bank", q, c] = product(held["weights", "we_mid"], c, held["x", q, MIDDLE])
+
+        def add_middle(q, c):
+            bank, index = held["mid_bank", q, c]
+            partial = new_tile("partial", [P, QUAD], F32, 2 * CHUNKS)
+            nc.vector.scalar_tensor_tensor(
+                out=partial[:], in0=bank[:], scalar=bias_cols[:, c, BE_ROW:BE_ROW + 1], in1=held["log", q, 0, c][:],
+                op0=ALU.add, op1=ALU.add)
+            free_banks.append(index)
+            held["partial", q, c] = partial
+
+        def turn_scores(q, j):
+            bank, index = take_bank()
+            for c in range(CHUNKS):
+                for i, source in enumerate((held["partial", q, c], held["log", q, 1, c])):
+                    nc.tensor.matmul(bank[:, c * P:(c + 1) * P], lhsT=source[:, j * P:(j + 1) * P], rhs=ident[:],
+                                     start=(i == 0), stop=(i == 1), is_transpose=True)
+            held["q_bank", q, j] = (bank, index)
+
+        def empty_scores(q, j):
+            if j == 0:
+                held["neg_q", q] = score_tile()
+                held["neg_top", q] = new_tile("neg_top", [P, TILES], F32, QUADS)
+            bank, index = held["q_bank", q, j]
+            nc.vector.tensor_scalar(out=held["neg_q", q][:, j, :], in0=bank[:], scalar1=-1.0, scalar2=None,
+                                    op0=ALU.mult, op1=ALU.min, accum_out=held["neg_top", q][:, j:j + 1])
+            free_banks.append(index)
+
+        def score_exp(q, j):
+            if j == 0:
+                held["total", q] = new_tile("total", [P, TILES], F32, QUADS)
+            unread = new_tile("unread", [P, T], BF16, 1)
+            nc.scalar.activation(out=unread[:], in_=held["neg_q", q][:, j, :], func=ACT.Exp, scale=-1.0,
+                                 bias=held["neg_top", q][:, j:j + 1], accum_out=held["total", q][:, j:j + 1])
+
+        def log_total(q):
+            log_mean = new_tile("log_mean", [P, TILES], F32, QUADS)
+            nc.scalar.activation(out=log_mean[:], in_=held["total", q][:], func=ACT.Ln, scale=1.0 / T)
+            held["log_mean", q] = log_mean
+
+        def make_shift(q):
+            shift = new_tile("shift", [P, TILES], F32, QUADS)
+            nc.vector.tensor_tensor(out=shift[:], in0=held["neg_top", q][:], in1=held["log_mean", q][:], op=ALU.subtract)
+            held["shift", q] = shift
+
+        def finish(q, j):
+            row = held["neg_q", q][:, j, :]
+            nc.vector.tensor_scalar(out=row, in0=row, scalar1=-1.0, scalar2=held["shift", q][:, j:j + 1], op0=ALU.mult, op1=ALU.add)
+            rows = out[q * QUAD:(q + 1) * QUAD, :].rearrange("(p j) t -> p j t", j=TILES)
+            nc.sync.dma_start(out=rows[:, j, :], in_=row)
+
+        events = []
+
+        def at(step, rank, call, *args):
+            events.append((step, rank, len(events), call, args))
+
+        def plan_x(q, due):
+            for l, first in ((NEIGHBOUR_OF[0], due - 14), (NEIGHBOUR_OF[1], due - 11), (MIDDLE, due - 9)):
+                if q > 0:
+                    at(first - 4, 0, load_bytes, q, l)
+                for h in range(2):
+                    at(first + h, 3, scale_x, q, l, h)
+                    at(first + h + 1, 8, turn_x, q, l, h)
+                    at(first + h + 2, 7, empty_x, q, l, h)
+                at(first + 4, 11, quantise_x, q, l)
+            for n in range(NB):
+                for c in range(CHUNKS):
+                    step = due - UNITS + n * CHUNKS + c
+                    at(step - 1, 12, multiply_neighbour, q, n, c)
+                    at(step, 4, empty_neighbour, q, n, c)
+
+        def plan_messages(q, base):
+            for n in range(NB):
+                for j in range(TILES):
+                    step = base + n * TILES + j
+                    at(step - 1, 2, turn_neighbour, q, n, j)
+                    if j % 2 == 0:
+                        at(step - 2, 12, turn_upper_halves, q, n, j // 2)
+                    at(step - 1 - j % 2, 6, neighbour_max, q, n, j)
+                    at(step, 1, neighbour_exp, q, n, j)
+                    at(step + 2, 9, apply_gain, q, n, j)
+                    if j % 2 == 1:
+                        at(step + 1, 2, reciprocals, q, n, j // 2)
+                        at(step + 3, 5, turn_v, q, n, j // 2)
+                        at(step + 3, 10, empty_v, q, n, j // 2)
+                at(base + (n + 1) * TILES + 3, 11, quantise_v, q, n)
+
+        def plan_logs(q, base):
+            for c in range(CHUNKS):
+                step = base + c
+                for n in range(NB):
+                    at(step, 5, multiply_message, q, n, c)
+                    at(step + 1, 3 + n, clamp, q, n, c)
+                    at(step + 2, 1 + n, log_message, q, n, c)
+                at(step + 2, 5, multiply_middle, q, c)
+                at(step + 3, 4, add_middle, q, c)
+            for j in range(TILES):
+                at(base + CHUNKS + 3 + j, 0, turn_scores, q, j)
+                at(base + CHUNKS + 3 + j, 8, empty_scores, q, j)
+
+        def plan_score_exps(quads, base, steps):
+            rows = [(q, j) for q in quads for j in range(TILES)]
+            for i, (q, j) in enumerate(rows):
+                at(base + i * steps // len(rows), 13, score_exp, q, j)
+
+        def plan_finish(quads, base, steps):
+            for q in quads:
+                at(base, 0, log_total, q)
+                at(base + 1, 0, make_shift, q)
+            rows = [(q, j) for q in quads for j in range(TILES)]
+            for i, (q, j) in enumerate(rows):
+                at(base + 1 + i * steps // len(rows), 9, finish, q, j)
+
+        at(-20, 0, load_constants)
+        at(-20, 1, make_constants)
+        at(-20, 2, make_scales)
+        at(-14, 5, interleave_we_permuted)
+        at(-13, 5, make_biases)
+        at(-12, 11, quantise_weights, "we_nb")
+        at(-12, 0, load_late_constants)
+        for n in range(NB):
+            at(-2 + n, 13, make_gains, n)
+            at(4 + 4 * n, 13, interleave_trans, n)
+            at(6 + 4 * n, 2, quantise_weights, ("trans", n))
+        at(0, 13, interleave_we)
+        at(2, 2, quantise_weights, "we_mid")
+
+        step = 0
+        first_quad = 0
+        previous = []
+        for size in GROUPS:
+            quads = list(range(first_quad, first_quad + size))
+            if previous:
+                plan_score_exps(previous, step + 1, size * UNITS - 1)
+            for q in quads:
+                if q == 0:
+                    plan_x(q, step)
+                plan_messages(q, step)
+                step = step + UNITS
+                if q + 1 < QUADS:
+                    plan_x(q + 1, step + (X_DELAY if q == quads[-1] else 0))
+            if previous:
+                plan_finish(previous, step, size * CHUNKS)
+            step = step - LOG_LEAD + max(0, LOG_LEAD + CHUNKS - (size - 1) * CHUNKS)
+            for q in quads:
+                plan_logs(q, step)
+                step = step + CHUNKS
+            step = step + GAP
+            previous = quads
+            first_quad = first_quad + size
+        plan_score_exps(previous, step + 1, len(previous) * TILES)
+        plan_finish(previous, step + 1 + len(previous) * TILES, 1)
+
+        for event in sorted(events, key=lambda event: event[0:3]):
+            event[3](*event[4])

@@ -14,7 +14,6 @@ FP8 = mybir.dt.float8_e4m3fn
 FP8X4 = mybir.dt.float8_e4m3fn_x4
 ALU = mybir.AluOpType
 ACT = mybir.ActivationFunctionType
-AXIS = mybir.AxisListType
 
 P = 128
 PACK = 4
@@ -22,17 +21,26 @@ QUAD = 512
 TILES = QUAD // P
 QUADS = B // QUAD
 CHUNKS = T // P
-UNITS = NB * TILES
 BANKS = 8
-GROUPS = (3, 3, 2)
-VECTOR_CLAMPS = 4
-VECTOR_EXITS = 1
-GAP = 2
-LOG_LEAD = 2
-X_DELAY = 8
-BE_ROW = 32
 NEIGHBOUR_OF = (0, 2)
 MIDDLE = 1
+BE_ROW = 32
+
+KNEE = 14.4
+SLOPE = 0.625
+
+GROUPS = (3, 3, 2)
+GROUP_MAX = max(GROUPS)
+
+EXP_STEPS = NB * TILES
+SCALE_STEPS = ((NEIGHBOUR_OF[0], (-12, -11)), (NEIGHBOUR_OF[1], (-10, -8)), (MIDDLE, (-7, -6)))
+LOAD_LEAD = 4
+EMPTY_FIRST = -6
+GAIN_LAG = 3
+LOG_LAG = 3
+X_DELAY = 12
+EARLY = 4
+FINISH_GAP = 3
 
 
 def tile_chunkflooredmessagemiddlescore_t_kernel(tc, x_bytes, x_scale, we, be, ends, gain, trans, out):
@@ -42,9 +50,8 @@ def tile_chunkflooredmessagemiddlescore_t_kernel(tc, x_bytes, x_scale, we, be, e
         ps = ctx.enter_context(tc.psum_pool(name="ps", bufs=1))
         ctx.enter_context(tc.manual_schedule())
 
-        group_max = max(GROUPS)
-        free_banks = list(range(BANKS))
         held = {}
+        free_banks = list(range(BANKS))
 
         def take_bank(dtype=F32, width=T):
             index = free_banks[0]
@@ -56,10 +63,13 @@ def tile_chunkflooredmessagemiddlescore_t_kernel(tc, x_bytes, x_scale, we, be, e
             return sb.tile(shape, dtype, tag=tag, name=tag, bufs=bufs, align_bytes=64)
 
         def interleaved_tile():
-            return new_tile("interleaved", [P, QUAD * PACK], BF16, 4)
+            return new_tile("interleaved", [P, QUAD * PACK], BF16, 5)
 
         def score_tile():
-            return new_tile("scores", [P, TILES, T], F32, group_max + 2)
+            return new_tile("scores", [P, TILES, T], F32, GROUP_MAX + 2)
+
+        def exp_tile():
+            return new_tile("exps", [P, T], F32, GAIN_LAG + 2)
 
         def quantise(source, tag, bufs):
             codes = new_tile(tag + "_codes", [P, QUAD], U32, bufs)
@@ -80,23 +90,25 @@ def tile_chunkflooredmessagemiddlescore_t_kernel(tc, x_bytes, x_scale, we, be, e
         scale_rows = new_tile("scale_rows", [P, 2, D], F32, 1)
         gain_rows = new_tile("gain_rows", [P, NB, T], F32, 1)
         bias_cols = new_tile("bias_cols", [P, CHUNKS, P], F32, 1)
-        offsets = new_tile("offsets", [P, 3], F32, 1)
+        one = new_tile("one", [P, 1], F32, 1)
+        knee = new_tile("knee", [P, 1], F32, 1)
 
         def load_bytes(q, l):
             raw = new_tile("x_raw", [P, TILES * D], U8, 4)
             rows = x_bytes[l, q * QUAD:(q + 1) * QUAD, :]
-            nc.sync.dma_start(out=raw[:], in_=rows.rearrange("(p j) k -> p (j k)", j=TILES))
+            nc.sync.dma_start(out=raw[:], in_=rows.rearrange("(r j) k -> r (j k)", j=TILES))
             held["raw", q, l] = raw
 
-        def load_constants():
+        def load_first():
             scale_cols = new_tile("scale_cols", [P, PACK], F32, 1)
             nc.sync.dma_start(out=scale_cols[:], in_=x_scale.rearrange("a b (p t) -> p (a b t)", t=PACK))
             held["scale_cols"] = scale_cols
             load_bytes(0, NEIGHBOUR_OF[0])
-            we_raw = score_tile()
-            we_view = we_raw[:].rearrange("p j t -> p (j t)").bitcast(BF16)[:, 0:PACK * T]
-            nc.sync.dma_start(out=we_view, in_=we.rearrange("(p j) n -> p (j n)", j=PACK))
-            held["we_raw"] = we_view
+            load_bytes(0, NEIGHBOUR_OF[1])
+            we_tile = score_tile()
+            we_raw = we_tile[:].rearrange("p j t -> p (j t)").bitcast(BF16)[:, 0:PACK * T]
+            nc.sync.dma_start(out=we_raw, in_=we.rearrange("(p t) n -> p (t n)", t=PACK))
+            held["we_raw"] = we_raw
             be_rows = new_tile("be_rows", [P, T], BF16, 1)
             end_rows = new_tile("end_rows", [P, T], BF16, 1)
             nc.sync.dma_start(out=be_rows[0:NB, :], in_=be.partition_broadcast(NB))
@@ -104,27 +116,23 @@ def tile_chunkflooredmessagemiddlescore_t_kernel(tc, x_bytes, x_scale, we, be, e
             nc.sync.dma_start(out=be_rows[BE_ROW:BE_ROW + 1, :], in_=be.rearrange("(o t) -> o t", o=1))
             held["be_rows"] = be_rows
             held["end_rows"] = end_rows
-            load_bytes(0, NEIGHBOUR_OF[1])
             load_bytes(0, MIDDLE)
-
-        def load_late_constants():
             gain_raw = new_tile("gain_raw", [P, NB, PACK], BF16, 1)
             nc.sync.dma_start(out=gain_raw[:], in_=gain.rearrange("n (p t) -> p n t", t=PACK))
             held["gain_raw"] = gain_raw
-            trans_raw = score_tile()
-            trans_view = trans_raw[:].rearrange("p j t -> p (j t)").bitcast(BF16).rearrange("p (n r) -> p n r", n=NB)
-            nc.sync.dma_start(out=trans_view, in_=trans.rearrange("n (p j) t -> p n (j t)", j=PACK))
-            held["trans_raw"] = trans_view
+            trans_tile = score_tile()
+            trans_raw = trans_tile[:].rearrange("p j t -> p (j t)").bitcast(BF16).rearrange("p (n r) -> p n r", n=NB)
+            nc.sync.dma_start(out=trans_raw, in_=trans.rearrange("n (p t) c -> p n (t c)", t=PACK))
+            held["trans_raw"] = trans_raw
 
         def make_constants():
             make_identity(nc, ident[:])
             make_identity(nc, ident_half[:])
-            bias_rows = new_tile("weights", [P, T], F32, 4)
+            bias_rows = exp_tile()
             nc.gpsimd.memset(bias_rows[:], 0.0)
-            nc.gpsimd.memset(offsets[:, 0:1], 9.0)
-            nc.gpsimd.memset(offsets[:, 1:2], 1.0)
-            nc.gpsimd.memset(offsets[:, 2:3], 10.0)
             held["bias_rows"] = bias_rows
+            nc.gpsimd.memset(one[:], 1.0)
+            nc.gpsimd.tensor_scalar(out=knee[:], in0=one[:], scalar1=KNEE, scalar2=0.0, op0=ALU.mult, op1=ALU.add)
 
         def spread(cols):
             bank, index = take_bank()
@@ -133,17 +141,18 @@ def tile_chunkflooredmessagemiddlescore_t_kernel(tc, x_bytes, x_scale, we, be, e
             return bank, index
 
         def make_scales():
-            bank, index = spread(held["scale_cols"])
-            nc.scalar.copy(out=scale_rows[:, 0, :].rearrange("r (p t) -> r p t", t=PACK), in_=bank[:].rearrange("r (t p) -> r p t", t=PACK))
-            nc.scalar.copy(out=scale_rows[:, 1, :], in_=scale_rows[:, 0, :])
-            free_banks.append(index)
+            for row, copy in enumerate((nc.scalar.copy, nc.vector.tensor_copy)):
+                bank, index = spread(held["scale_cols"])
+                copy(out=scale_rows[:, row, :].rearrange("r (p t) -> r p t", t=PACK),
+                     in_=bank[:].rearrange("r (t p) -> r p t", t=PACK))
+                free_banks.append(index)
 
         def make_biases():
             bias_rows = held["bias_rows"]
             nc.vector.tensor_tensor(
-                out=bias_rows[0:NB, :].rearrange("r (u p e) -> r u p e", u=2, e=2),
-                in0=held["be_rows"][0:NB, :].rearrange("r (p u e) -> r u p e", u=2, e=2),
-                in1=held["end_rows"][0:NB, :].rearrange("r (p u e) -> r u p e", u=2, e=2), op=ALU.add)
+                out=bias_rows[0:NB, :].rearrange("n (u p e) -> n u p e", u=2, e=2),
+                in0=held["be_rows"][0:NB, :].rearrange("n (p u e) -> n u p e", u=2, e=2),
+                in1=held["end_rows"][0:NB, :].rearrange("n (p u e) -> n u p e", u=2, e=2), op=ALU.add)
             nc.vector.tensor_copy(out=bias_rows[BE_ROW:BE_ROW + 1, :], in_=held["be_rows"][BE_ROW:BE_ROW + 1, :])
             bank, index = take_bank()
             for c in range(CHUNKS):
@@ -159,23 +168,22 @@ def tile_chunkflooredmessagemiddlescore_t_kernel(tc, x_bytes, x_scale, we, be, e
                            in_=bank[:].rearrange("r (u e p) -> r u p e", u=2, e=2))
             free_banks.append(index)
 
-        def interleave_we_permuted():
+        def interleave_we_paired():
             grouped = interleaved_tile()
-            nc.scalar.copy(
-                out=grouped[:].rearrange("r (u p e j) -> r u p e j", u=2, e=2, j=PACK),
-                in_=held["we_raw"].rearrange("r (j p u e) -> r u p e j", j=PACK, u=2, e=2))
-            held["grouped", "we_nb"] = grouped
+            nc.scalar.copy(out=grouped[:].rearrange("r (u p e t) -> r u p e t", u=2, e=2, t=PACK),
+                           in_=held["we_raw"].rearrange("r (t p u e) -> r u p e t", t=PACK, u=2, e=2))
+            held["grouped", "we_paired"] = grouped
 
-        def interleave_natural(key, raw):
+        def interleave_plain(key, raw, copy):
             grouped = interleaved_tile()
-            nc.scalar.copy(out=grouped[:].rearrange("r (n j) -> r n j", j=PACK), in_=raw.rearrange("r (j n) -> r n j", j=PACK))
+            copy(out=grouped[:].rearrange("r (c t) -> r c t", t=PACK), in_=raw.rearrange("r (t c) -> r c t", t=PACK))
             held["grouped", key] = grouped
 
-        def interleave_we():
-            interleave_natural("we_mid", held["we_raw"])
+        def interleave_we_plain():
+            interleave_plain("we_plain", held["we_raw"], nc.vector.tensor_copy)
 
         def interleave_trans(n):
-            interleave_natural(("trans", n), held["trans_raw"][:, n, :])
+            interleave_plain(("trans", n), held["trans_raw"][:, n, :], nc.scalar.copy)
 
         def quantise_weights(key):
             held["weights", key] = quantise(held["grouped", key], "w", 2 + NB)
@@ -192,9 +200,8 @@ def tile_chunkflooredmessagemiddlescore_t_kernel(tc, x_bytes, x_scale, we, be, e
             bank, index = take_bank()
             for j in range(2):
                 for u in range(2):
-                    nc.tensor.transpose(
-                        bank[:, (2 * j + u) * P:(2 * j + u + 1) * P],
-                        words[:, j * 2 * P + u:(j + 1) * 2 * P:2], ident[:])
+                    nc.tensor.transpose(bank[:, (2 * j + u) * P:(2 * j + u + 1) * P],
+                                        words[:, j * 2 * P + u:(j + 1) * 2 * P:2], ident[:])
             held["x_bank", q, l, h] = (bank, index)
 
         def empty_words(bank_key, grouped_key, h):
@@ -202,9 +209,8 @@ def tile_chunkflooredmessagemiddlescore_t_kernel(tc, x_bytes, x_scale, we, be, e
                 held[grouped_key] = interleaved_tile()
             bank, index = held[bank_key]
             words = held[grouped_key][:].bitcast(F32)[:, h * T:(h + 1) * T]
-            nc.scalar.copy(
-                out=words.rearrange("p (j r u) -> p j r u", j=2, u=2),
-                in_=bank[:].rearrange("p (j u r) -> p j r u", j=2, u=2))
+            nc.scalar.copy(out=words.rearrange("p (j r u) -> p j r u", j=2, u=2),
+                           in_=bank[:].rearrange("p (j u r) -> p j r u", j=2, u=2))
             free_banks.append(index)
 
         def empty_x(q, l, h):
@@ -212,35 +218,26 @@ def tile_chunkflooredmessagemiddlescore_t_kernel(tc, x_bytes, x_scale, we, be, e
 
         def quantise_x(q, l):
             if l == MIDDLE:
-                held["x", q, l] = quantise(held["x_grouped", q, l], "x_mid", group_max + 2)
+                held["x", q, l] = quantise(held["x_grouped", q, l], "x_middle", GROUP_MAX + 2)
             else:
-                held["x", q, l] = quantise(held["x_grouped", q, l], "x_nb", 2)
+                held["x", q, l] = quantise(held["x_grouped", q, l], "x_neighbour", 2)
 
         def multiply_neighbour(q, n, c):
-            held["e_bank", q, n, c] = product(held["weights", "we_nb"], c, held["x", q, NEIGHBOUR_OF[n]])
+            held["e_bank", q, n, c] = product(held["weights", "we_paired"], c, held["x", q, NEIGHBOUR_OF[n]])
 
         def empty_neighbour(q, n, c):
             if c == 0:
-                held["n_t", q, n] = new_tile("n_t", [P, CHUNKS, QUAD], F32, 4)
+                held["n_tags", q, n] = new_tile("n_tags", [P, CHUNKS, QUAD], F32, 3)
             bank, index = held["e_bank", q, n, c]
-            if n * CHUNKS + c < VECTOR_EXITS:
-                nc.vector.tensor_scalar(out=held["n_t", q, n][:, c, :], in0=bank[:], scalar1=bias_cols[:, c, n:n + 1], scalar2=None, op0=ALU.add)
-            else:
-                nc.scalar.activation(out=held["n_t", q, n][:, c, :], in_=bank[:], func=ACT.Identity, bias=bias_cols[:, c, n:n + 1])
+            nc.scalar.activation(out=held["n_tags", q, n][:, c, :], in_=bank[:], func=ACT.Identity, bias=bias_cols[:, c, n:n + 1])
             free_banks.append(index)
-
-        def turn_neighbour(q, n, j):
-            bank, index = take_bank()
-            for c in range(CHUNKS):
-                nc.tensor.transpose(bank[:, c * P:(c + 1) * P], held["n_t", q, n][:, c, j * P:(j + 1) * P], ident[:])
-            held["n_bank", q, n, j] = (bank, index)
 
         def turn_upper_halves(q, n, h):
             bank, index = take_bank(BF16, 2 * T)
             for i in range(2):
                 j = 2 * h + i
                 for c in range(CHUNKS):
-                    halves = held["n_t", q, n][:, c, :].bitcast(BF16)
+                    halves = held["n_tags", q, n][:, c, :].bitcast(BF16)
                     nc.tensor.transpose(bank[:, i * T + c * P:i * T + (c + 1) * P],
                                         halves[:, 2 * j * P + 1:2 * (j + 1) * P:2], ident_half[:])
             held["top_bank", q, n, h] = (bank, index)
@@ -249,21 +246,27 @@ def tile_chunkflooredmessagemiddlescore_t_kernel(tc, x_bytes, x_scale, we, be, e
             if j == 0:
                 held["neg_max", q, n] = new_tile("neg_max", [P, TILES], F32, 3)
             bank, index = held["top_bank", q, n, j // 2]
-            negated = new_tile("negated", [P, T], BF16, 1)
+            negated = new_tile("negated", [P, T], BF16, 2)
             nc.vector.tensor_scalar(out=negated[:], in0=bank[:, (j % 2) * T:(j % 2 + 1) * T], scalar1=-1.0, scalar2=None,
                                     op0=ALU.mult, op1=ALU.min, accum_out=held["neg_max", q, n][:, j:j + 1])
             if j % 2 == 1:
                 free_banks.append(index)
 
+        def turn_neighbour(q, n, j):
+            bank, index = take_bank()
+            for c in range(CHUNKS):
+                nc.tensor.transpose(bank[:, c * P:(c + 1) * P], held["n_tags", q, n][:, c, j * P:(j + 1) * P], ident[:])
+            held["n_bank", q, n, j] = (bank, index)
+
         def neighbour_exp(q, n, j):
             if j == 0:
                 held["sums", q, n] = new_tile("sums", [P, TILES], F32, 3)
             bank, index = held["n_bank", q, n, j]
-            w = new_tile("weights", [P, T], F32, 4)
-            nc.scalar.activation(out=w[:], in_=bank[:], func=ACT.Exp, bias=held["neg_max", q, n][:, j:j + 1],
+            exps = exp_tile()
+            nc.scalar.activation(out=exps[:], in_=bank[:], func=ACT.Exp, bias=held["neg_max", q, n][:, j:j + 1],
                                  accum_out=held["sums", q, n][:, j:j + 1])
             free_banks.append(index)
-            held["w", q, n, j] = w
+            held["exps", q, n, j] = exps
 
         def reciprocals(q, n, h):
             if h == 0:
@@ -274,13 +277,13 @@ def tile_chunkflooredmessagemiddlescore_t_kernel(tc, x_bytes, x_scale, we, be, e
             if j % 2 == 0:
                 held["v", q, n, j // 2] = new_tile("v", [P, 2, T], BF16, 2)
             nc.vector.scalar_tensor_tensor(
-                out=held["v", q, n, j // 2][:, j % 2, :], in0=held["w", q, n, j][:], scalar=held["recip", q, n][:, j:j + 1],
+                out=held["v", q, n, j // 2][:, j % 2, :], in0=held["exps", q, n, j][:], scalar=held["recip", q, n][:, j:j + 1],
                 in1=gain_rows[:, n, :], op0=ALU.mult, op1=ALU.mult)
 
         def turn_v(q, n, h):
             words = held["v", q, n, h][:].rearrange("p j t -> p (j t)").bitcast(F32)
             bank, index = take_bank()
-            for i in range(4):
+            for i in range(2 * 2):
                 nc.tensor.transpose(bank[:, i * P:(i + 1) * P], words[:, i * P:(i + 1) * P], ident[:])
             held["v_bank", q, n, h] = (bank, index)
 
@@ -288,65 +291,58 @@ def tile_chunkflooredmessagemiddlescore_t_kernel(tc, x_bytes, x_scale, we, be, e
             empty_words(("v_bank", q, n, h), ("v_grouped", q, n), h)
 
         def quantise_v(q, n):
-            held["v_codes", q, n] = quantise(held["v_grouped", q, n], "v", NB * group_max + 1)
+            held["v_codes", q, n] = quantise(held["v_grouped", q, n], "v", NB * GROUP_MAX + 1)
 
         def multiply_message(q, n, c):
             held["m_bank", q, n, c] = product(held["weights", ("trans", n)], c, held["v_codes", q, n])
 
-        def clamp(q, n, c):
+        def floor_message(q, n, c):
             bank, index = held["m_bank", q, n, c]
-            floored = new_tile("floored", [P, QUAD], F32, 4)
-            if n * CHUNKS + c < VECTOR_CLAMPS:
-                nc.vector.tensor_scalar(out=floored[:], in0=bank[:], scalar1=0.625, scalar2=-9.0, op0=ALU.mult, op1=ALU.max)
-                held["floored", q, n, c] = (floored, offsets[:, 2:3])
+            if n == 0:
+                held["floored", q, c] = new_tile("floored", [P, NB, QUAD], F32, LOG_LAG + EARLY // 2)
+                nc.vector.tensor_scalar(out=held["floored", q, c][:, n, :], in0=bank[:], scalar1=KNEE, scalar2=0.0,
+                                        op0=ALU.add, op1=ALU.max)
             else:
-                nc.scalar.activation(out=floored[:], in_=bank[:], func=ACT.Relu, scale=0.625, bias=offsets[:, 0:1])
-                held["floored", q, n, c] = (floored, offsets[:, 1:2])
+                nc.scalar.activation(out=held["floored", q, c][:, n, :], in_=bank[:], func=ACT.Relu, bias=knee[:])
             free_banks.append(index)
 
-        def log_message(q, n, c):
-            floored, offset = held["floored", q, n, c]
-            if n == 0:
-                logs = new_tile("log_first", [P, QUAD], F32, 3)
-            else:
-                logs = new_tile("log_second", [P, QUAD], F32, 2 * CHUNKS)
-            nc.scalar.activation(out=logs[:], in_=floored[:], func=ACT.Ln, bias=offset)
-            held["log", q, n, c] = logs
+        def log_messages(q, c):
+            logs = new_tile("logs", [P, NB, QUAD], F32, 2 * CHUNKS + 1)
+            nc.scalar.activation(out=logs[:], in_=held["floored", q, c][:], func=ACT.Ln, scale=SLOPE, bias=one[:])
+            held["logs", q, c] = logs
 
         def multiply_middle(q, c):
-            held["mid_bank", q, c] = product(held["weights", "we_mid"], c, held["x", q, MIDDLE])
+            held["middle_bank", q, c] = product(held["weights", "we_plain"], c, held["x", q, MIDDLE])
 
         def add_middle(q, c):
-            bank, index = held["mid_bank", q, c]
-            partial = new_tile("partial", [P, QUAD], F32, 2 * CHUNKS)
-            nc.vector.scalar_tensor_tensor(
-                out=partial[:], in0=bank[:], scalar=bias_cols[:, c, BE_ROW:BE_ROW + 1], in1=held["log", q, 0, c][:],
-                op0=ALU.add, op1=ALU.add)
+            bank, index = held["middle_bank", q, c]
+            first_log = held["logs", q, c][:, 0, :]
+            nc.vector.scalar_tensor_tensor(out=first_log, in0=bank[:], scalar=bias_cols[:, c, BE_ROW:BE_ROW + 1], in1=first_log,
+                                           op0=ALU.add, op1=ALU.add)
             free_banks.append(index)
-            held["partial", q, c] = partial
 
         def turn_scores(q, j):
             bank, index = take_bank()
             for c in range(CHUNKS):
-                for i, source in enumerate((held["partial", q, c], held["log", q, 1, c])):
-                    nc.tensor.matmul(bank[:, c * P:(c + 1) * P], lhsT=source[:, j * P:(j + 1) * P], rhs=ident[:],
-                                     start=(i == 0), stop=(i == 1), is_transpose=True)
-            held["q_bank", q, j] = (bank, index)
+                for n in range(NB):
+                    nc.tensor.matmul(bank[:, c * P:(c + 1) * P], lhsT=held["logs", q, c][:, n, j * P:(j + 1) * P], rhs=ident[:],
+                                     start=(n == 0), stop=(n == NB - 1), is_transpose=True)
+            held["score_bank", q, j] = (bank, index)
 
         def empty_scores(q, j):
             if j == 0:
-                held["neg_q", q] = score_tile()
+                held["neg_scores", q] = score_tile()
                 held["neg_top", q] = new_tile("neg_top", [P, TILES], F32, QUADS)
-            bank, index = held["q_bank", q, j]
-            nc.vector.tensor_scalar(out=held["neg_q", q][:, j, :], in0=bank[:], scalar1=-1.0, scalar2=None,
+            bank, index = held["score_bank", q, j]
+            nc.vector.tensor_scalar(out=held["neg_scores", q][:, j, :], in0=bank[:], scalar1=-1.0, scalar2=None,
                                     op0=ALU.mult, op1=ALU.min, accum_out=held["neg_top", q][:, j:j + 1])
             free_banks.append(index)
 
         def score_exp(q, j):
             if j == 0:
                 held["total", q] = new_tile("total", [P, TILES], F32, QUADS)
-            unread = new_tile("unread", [P, T], BF16, 1)
-            nc.scalar.activation(out=unread[:], in_=held["neg_q", q][:, j, :], func=ACT.Exp, scale=-1.0,
+            terms = new_tile("terms", [P, T], BF16, 2)
+            nc.scalar.activation(out=terms[:], in_=held["neg_scores", q][:, j, :], func=ACT.Exp, scale=-1.0,
                                  bias=held["neg_top", q][:, j:j + 1], accum_out=held["total", q][:, j:j + 1])
 
         def log_total(q):
@@ -359,30 +355,30 @@ def tile_chunkflooredmessagemiddlescore_t_kernel(tc, x_bytes, x_scale, we, be, e
             nc.vector.tensor_tensor(out=shift[:], in0=held["neg_top", q][:], in1=held["log_mean", q][:], op=ALU.subtract)
             held["shift", q] = shift
 
-        def finish(q, j):
-            row = held["neg_q", q][:, j, :]
-            nc.vector.tensor_scalar(out=row, in0=row, scalar1=-1.0, scalar2=held["shift", q][:, j:j + 1], op0=ALU.mult, op1=ALU.add)
-            rows = out[q * QUAD:(q + 1) * QUAD, :].rearrange("(p j) t -> p j t", j=TILES)
+        def finish(q, j, engine):
+            row = held["neg_scores", q][:, j, :]
+            engine.tensor_scalar(out=row, in0=row, scalar1=-1.0, scalar2=held["shift", q][:, j:j + 1], op0=ALU.mult, op1=ALU.add)
+            rows = out[q * QUAD:(q + 1) * QUAD, :].rearrange("(r j) t -> r j t", j=TILES)
             nc.sync.dma_start(out=rows[:, j, :], in_=row)
 
         events = []
 
-        def at(step, rank, call, *args):
-            events.append((step, rank, len(events), call, args))
+        def at(step, place, call, *args):
+            events.append((step, place, len(events), call, args))
 
         def plan_x(q, due):
-            for l, first in ((NEIGHBOUR_OF[0], due - 14), (NEIGHBOUR_OF[1], due - 11), (MIDDLE, due - 9)):
+            for l, offsets in SCALE_STEPS:
                 if q > 0:
-                    at(first - 4, 0, load_bytes, q, l)
+                    at(due + offsets[0] - LOAD_LEAD, 0, load_bytes, q, l)
                 for h in range(2):
-                    at(first + h, 3, scale_x, q, l, h)
-                    at(first + h + 1, 8, turn_x, q, l, h)
-                    at(first + h + 2, 7, empty_x, q, l, h)
-                at(first + 4, 11, quantise_x, q, l)
+                    at(due + offsets[h], 3, scale_x, q, l, h)
+                    at(due + offsets[h] + 1, 8, turn_x, q, l, h)
+                    at(due + offsets[h] + 2, 7, empty_x, q, l, h)
+                at(due + offsets[1] + 3, 11, quantise_x, q, l)
             for n in range(NB):
                 for c in range(CHUNKS):
-                    step = due - UNITS + n * CHUNKS + c
-                    at(step - 1, 12, multiply_neighbour, q, n, c)
+                    step = due + EMPTY_FIRST + n * CHUNKS + c
+                    at(step - 1 - c % 2, 12, multiply_neighbour, q, n, c)
                     at(step, 4, empty_neighbour, q, n, c)
 
         def plan_messages(q, base):
@@ -394,78 +390,77 @@ def tile_chunkflooredmessagemiddlescore_t_kernel(tc, x_bytes, x_scale, we, be, e
                         at(step - 2, 12, turn_upper_halves, q, n, j // 2)
                     at(step - 1 - j % 2, 6, neighbour_max, q, n, j)
                     at(step, 1, neighbour_exp, q, n, j)
-                    at(step + 2, 9, apply_gain, q, n, j)
+                    at(step + GAIN_LAG, 9, apply_gain, q, n, j)
                     if j % 2 == 1:
-                        at(step + 1, 2, reciprocals, q, n, j // 2)
-                        at(step + 3, 5, turn_v, q, n, j // 2)
-                        at(step + 3, 10, empty_v, q, n, j // 2)
-                at(base + (n + 1) * TILES + 3, 11, quantise_v, q, n)
+                        at(step + 1, 10, reciprocals, q, n, j // 2)
+                        at(step + GAIN_LAG + 1, 5, turn_v, q, n, j // 2)
+                        at(step + GAIN_LAG + 1, 10, empty_v, q, n, j // 2)
+                at(base + (n + 1) * TILES + GAIN_LAG + 1, 11, quantise_v, q, n)
 
-        def plan_logs(q, base):
+        def plan_logs(q, base, group_base):
             for c in range(CHUNKS):
                 step = base + c
+                early = max(0, EARLY - (step - group_base))
                 for n in range(NB):
-                    at(step, 5, multiply_message, q, n, c)
-                    at(step + 1, 3 + n, clamp, q, n, c)
-                    at(step + 2, 1 + n, log_message, q, n, c)
-                at(step + 2, 5, multiply_middle, q, c)
-                at(step + 3, 4, add_middle, q, c)
+                    at(step - early, 5, multiply_message, q, n, c)
+                    at(step - early + 1, 3 + n, floor_message, q, n, c)
+                at(step + LOG_LAG, 1, log_messages, q, c)
+                at(step + LOG_LAG, 5, multiply_middle, q, c)
+                at(step + LOG_LAG + 1, 4, add_middle, q, c)
             for j in range(TILES):
-                at(base + CHUNKS + 3 + j, 0, turn_scores, q, j)
-                at(base + CHUNKS + 3 + j, 8, empty_scores, q, j)
+                at(base + CHUNKS + LOG_LAG + 1 + j, 0, turn_scores, q, j)
+                at(base + CHUNKS + LOG_LAG + 1 + j, 8, empty_scores, q, j)
 
         def plan_score_exps(quads, base, steps):
             rows = [(q, j) for q in quads for j in range(TILES)]
             for i, (q, j) in enumerate(rows):
                 at(base + i * steps // len(rows), 13, score_exp, q, j)
 
-        def plan_finish(quads, base, steps):
-            for q in quads:
-                at(base, 0, log_total, q)
-                at(base + 1, 0, make_shift, q)
-            rows = [(q, j) for q in quads for j in range(TILES)]
-            for i, (q, j) in enumerate(rows):
-                at(base + 1 + i * steps // len(rows), 9, finish, q, j)
+        def plan_finish(quads, base, gap, engine):
+            for i, q in enumerate(quads):
+                at(base + i * gap, 0, log_total, q)
+                at(base + i * gap + 1, 0, make_shift, q)
+                for j in range(TILES):
+                    at(base + i * gap + 1, 9, finish, q, j, engine)
 
-        at(-20, 0, load_constants)
-        at(-20, 1, make_constants)
-        at(-20, 2, make_scales)
-        at(-14, 5, interleave_we_permuted)
-        at(-13, 5, make_biases)
-        at(-12, 11, quantise_weights, "we_nb")
-        at(-12, 0, load_late_constants)
+        head = SCALE_STEPS[0][1][0] - LOAD_LEAD
+        first_copy = SCALE_STEPS[0][1][0] + 2
+        at(head, 0, load_first)
+        at(head, 1, make_constants)
+        at(head, 2, make_scales)
+        at(first_copy, 5, interleave_we_paired)
+        at(first_copy + 1, 5, make_biases)
+        at(first_copy + 1, 11, quantise_weights, "we_paired")
+        at(first_copy + 1, 13, interleave_we_plain)
+        at(first_copy + 4, 13, quantise_weights, "we_plain")
         for n in range(NB):
-            at(-2 + n, 13, make_gains, n)
-            at(4 + 4 * n, 13, interleave_trans, n)
-            at(6 + 4 * n, 2, quantise_weights, ("trans", n))
-        at(0, 13, interleave_we)
-        at(2, 2, quantise_weights, "we_mid")
+            at(first_copy + 3 * (n + 1), 13, interleave_trans, n)
+            at(first_copy + 3 * (n + 2), 13, quantise_weights, ("trans", n))
+            at(n - NB, 13, make_gains, n)
 
+        plan_x(0, 0)
         step = 0
-        first_quad = 0
         previous = []
-        for size in GROUPS:
-            quads = list(range(first_quad, first_quad + size))
+        for g, size in enumerate(GROUPS):
+            quads = list(range(sum(GROUPS[0:g]), sum(GROUPS[0:g + 1])))
             if previous:
-                plan_score_exps(previous, step + 1, size * UNITS - 1)
+                plan_score_exps(previous, step + 1, size * EXP_STEPS - 1)
             for q in quads:
-                if q == 0:
-                    plan_x(q, step)
                 plan_messages(q, step)
-                step = step + UNITS
+                step = step + EXP_STEPS
                 if q + 1 < QUADS:
                     plan_x(q + 1, step + (X_DELAY if q == quads[-1] else 0))
             if previous:
-                plan_finish(previous, step, size * CHUNKS)
-            step = step - LOG_LEAD + max(0, LOG_LEAD + CHUNKS - (size - 1) * CHUNKS)
+                plan_finish(previous, step + FINISH_GAP, FINISH_GAP, nc.gpsimd)
+            step = max(step - LOG_LAG, step + GAIN_LAG + 2 - (size - 1) * CHUNKS)
+            group_base = step
             for q in quads:
-                plan_logs(q, step)
+                plan_logs(q, step, group_base)
                 step = step + CHUNKS
-            step = step + GAP
+            step = step + LOG_LAG
             previous = quads
-            first_quad = first_quad + size
         plan_score_exps(previous, step + 1, len(previous) * TILES)
-        plan_finish(previous, step + 1 + len(previous) * TILES, 1)
+        plan_finish(previous, step + 1 + len(previous) * TILES, 0, nc.vector)
 
-        for event in sorted(events, key=lambda event: event[0:3]):
+        for event in sorted(events, key=lambda entry: entry[0:3]):
             event[3](*event[4])

from contextlib import ExitStack

import concourse.mybir as mybir
from concourse.masks import make_identity

L, NB, B, D, T = 3, 2, 4096, 512, 512
FLOPS = 2 * (L + NB) * B * D * T

F32 = mybir.dt.float32
BF16 = mybir.dt.bfloat16
U32 = mybir.dt.uint32
U8 = mybir.dt.uint8
FP8 = mybir.dt.float8_e4m3fn
FP8X4 = mybir.dt.float8_e4m3fn_x4
ALU = mybir.AluOpType
ACT = mybir.ActivationFunctionType

P = 128
PACK = 4
QUAD = 512
TILES = QUAD // P
QUADS = B // QUAD
CHUNKS = T // P
BANKS = 8
NEIGHBOUR_OF = (0, 2)
MIDDLE = 1
BE_ROW = 32

KNEE = 14.4
SLOPE = 0.625

GROUPS = (3, 3, 2)
GROUP_MAX = max(GROUPS)

EXP_STEPS = NB * TILES
SCALE_STEPS = ((NEIGHBOUR_OF[0], (-12, -11)), (NEIGHBOUR_OF[1], (-10, -8)), (MIDDLE, (-7, -6)))
LOAD_LEAD = 4
EMPTY_FIRST = -6
GAIN_LAG = 3
LOG_LAG = 3
X_DELAY = 12
EARLY = 4
FINISH_GAP = 3


def tile_chunkflooredmessagemiddlescore_t_kernel(tc, x_bytes, x_scale, we, be, ends, gain, trans, out):
    nc = tc.nc
    with ExitStack() as ctx:
        sb = ctx.enter_context(tc.tile_pool(name="sb", bufs=1))
        ps = ctx.enter_context(tc.psum_pool(name="ps", bufs=1))
        ctx.enter_context(tc.manual_schedule())

        held = {}
        free_banks = list(range(BANKS))

        def take_bank(dtype=F32, width=T):
            index = free_banks[0]
            free_banks.remove(index)
            bank = ps.tile([P, width], dtype, tag="bank%d" % index, name="bank%d" % index)
            return bank, index

        def new_tile(tag, shape, dtype, bufs):
            return sb.tile(shape, dtype, tag=tag, name=tag, bufs=bufs, align_bytes=64)

        def interleaved_tile():
            return new_tile("interleaved", [P, QUAD * PACK], BF16, 5)

        def score_tile():
            return new_tile("scores", [P, TILES, T], F32, GROUP_MAX + 2)

        def exp_tile():
            return new_tile("exps", [P, T], F32, GAIN_LAG + 2)

        def quantise(source, tag, bufs):
            codes = new_tile(tag + "_codes", [P, QUAD], U32, bufs)
            scales = new_tile(tag + "_scales", [P, QUAD], U8, bufs)
            nc.vector.quantize_mx(out=codes[:].bitcast(FP8X4), scales=scales[:], in_=source[:])
            return codes, scales

        def product(weights, c, moving):
            bank, index = take_bank()
            cols = slice(c * P, (c + 1) * P)
            nc.tensor.matmul_mx(
                out=bank[:], lhsT=weights[0][:, cols].bitcast(FP8X4), lhsT_scale=weights[1][:, cols],
                rhs=moving[0][:].bitcast(FP8X4), rhs_scale=moving[1][:], start=True, stop=True)
            return bank, index

        ident = new_tile("ident", [P, P], F32, 1)
        ident_half = new_tile("ident_half", [P, P], BF16, 1)
        scale_rows = new_tile("scale_rows", [P, 2, D], F32, 1)
        gain_rows = new_tile("gain_rows", [P, NB, T], F32, 1)
        bias_cols = new_tile("bias_cols", [P, CHUNKS, P], F32, 1)
        one = new_tile("one", [P, 1], F32, 1)
        knee = new_tile("knee", [P, 1], F32, 1)

        def load_bytes(q, l):
            raw = new_tile("x_raw", [P, TILES * D], U8, 4)
            rows = x_bytes[l, q * QUAD:(q + 1) * QUAD, :]
            nc.sync.dma_start(out=raw[:], in_=rows.rearrange("(r j) k -> r (j k)", j=TILES))
            held["raw", q, l] = raw

        def load_first():
            scale_cols = new_tile("scale_cols", [P, PACK], F32, 1)
            nc.sync.dma_start(out=scale_cols[:], in_=x_scale.rearrange("a b (p t) -> p (a b t)", t=PACK))
            held["scale_cols"] = scale_cols
            load_bytes(0, NEIGHBOUR_OF[0])
            load_bytes(0, NEIGHBOUR_OF[1])
            we_tile = score_tile()
            we_raw = we_tile[:].rearrange("p j t -> p (j t)").bitcast(BF16)[:, 0:PACK * T]
            nc.sync.dma_start(out=we_raw, in_=we.rearrange("(p t) n -> p (t n)", t=PACK))
            held["we_raw"] = we_raw
            be_rows = new_tile("be_rows", [P, T], BF16, 1)
            end_rows = new_tile("end_rows", [P, T], BF16, 1)
            nc.sync.dma_start(out=be_rows[0:NB, :], in_=be.partition_broadcast(NB))
            nc.sync.dma_start(out=end_rows[0:NB, :], in_=ends)
            nc.sync.dma_start(out=be_rows[BE_ROW:BE_ROW + 1, :], in_=be.rearrange("(o t) -> o t", o=1))
            held["be_rows"] = be_rows
            held["end_rows"] = end_rows
            load_bytes(0, MIDDLE)
            gain_raw = new_tile("gain_raw", [P, NB, PACK], BF16, 1)
            nc.sync.dma_start(out=gain_raw[:], in_=gain.rearrange("n (p t) -> p n t", t=PACK))
            held["gain_raw"] = gain_raw
            trans_tile = score_tile()
            trans_raw = trans_tile[:].rearrange("p j t -> p (j t)").bitcast(BF16).rearrange("p (n r) -> p n r", n=NB)
            nc.sync.dma_start(out=trans_raw, in_=trans.rearrange("n (p t) c -> p n (t c)", t=PACK))
            held["trans_raw"] = trans_raw

        def make_constants():
            make_identity(nc, ident[:])
            make_identity(nc, ident_half[:])
            bias_rows = exp_tile()
            nc.gpsimd.memset(bias_rows[:], 0.0)
            held["bias_rows"] = bias_rows
            nc.gpsimd.memset(one[:], 1.0)
            nc.gpsimd.tensor_scalar(out=knee[:], in0=one[:], scalar1=KNEE, scalar2=0.0, op0=ALU.mult, op1=ALU.add)

        def spread(cols):
            bank, index = take_bank()
            for t in range(PACK):
                nc.tensor.transpose(bank[:, t * P:(t + 1) * P], cols[:, t:t + 1].to_broadcast([P, P]), ident[:])
            return bank, index

        def make_scales():
            for row, copy in enumerate((nc.scalar.copy, nc.vector.tensor_copy)):
                bank, index = spread(held["scale_cols"])
                copy(out=scale_rows[:, row, :].rearrange("r (p t) -> r p t", t=PACK),
                     in_=bank[:].rearrange("r (t p) -> r p t", t=PACK))
                free_banks.append(index)

        def make_biases():
            bias_rows = held["bias_rows"]
            nc.vector.tensor_tensor(
                out=bias_rows[0:NB, :].rearrange("n (u p e) -> n u p e", u=2, e=2),
                in0=held["be_rows"][0:NB, :].rearrange("n (p u e) -> n u p e", u=2, e=2),
                in1=held["end_rows"][0:NB, :].rearrange("n (p u e) -> n u p e", u=2, e=2), op=ALU.add)
            nc.vector.tensor_copy(out=bias_rows[BE_ROW:BE_ROW + 1, :], in_=held["be_rows"][BE_ROW:BE_ROW + 1, :])
            bank, index = take_bank()
            for c in range(CHUNKS):
                nc.tensor.transpose(bank[:, c * P:(c + 1) * P], bias_rows[:, c * P:(c + 1) * P], ident[:])
            nc.scalar.copy(out=bias_cols[:].rearrange("p c r -> p (c r)"), in_=bank[:])
            free_banks.append(index)

        def make_gains(n):
            gain_cols = new_tile("gain_cols", [P, PACK], F32, NB)
            nc.vector.tensor_scalar(out=gain_cols[:], in0=held["gain_raw"][:, n, :], scalar1=float(T), scalar2=None, op0=ALU.mult)
            bank, index = spread(gain_cols)
            nc.scalar.copy(out=gain_rows[:, n, :].rearrange("r (u p e) -> r u p e", u=2, e=2),
                           in_=bank[:].rearrange("r (u e p) -> r u p e", u=2, e=2))
            free_banks.append(index)

        def interleave_we_paired():
            grouped = interleaved_tile()
            nc.scalar.copy(out=grouped[:].rearrange("r (u p e t) -> r u p e t", u=2, e=2, t=PACK),
                           in_=held["we_raw"].rearrange("r (t p u e) -> r u p e t", t=PACK, u=2, e=2))
            held["grouped", "we_paired"] = grouped

        def interleave_plain(key, raw, copy):
            grouped = interleaved_tile()
            copy(out=grouped[:].rearrange("r (c t) -> r c t", t=PACK), in_=raw.rearrange("r (t c) -> r c t", t=PACK))
            held["grouped", key] = grouped

        def interleave_we_plain():
            interleave_plain("we_plain", held["we_raw"], nc.vector.tensor_copy)

        def interleave_trans(n):
            interleave_plain(("trans", n), held["trans_raw"][:, n, :], nc.scalar.copy)

        def quantise_weights(key):
            held["weights", key] = quantise(held["grouped", key], "w", 2 + NB)

        def scale_x(q, l, h):
            scaled = new_tile("scaled", [P, 2 * D], BF16, 3)
            nc.vector.tensor_tensor(
                out=scaled[:], in0=held["raw", q, l][:, h * 2 * D:(h + 1) * 2 * D].bitcast(FP8),
                in1=scale_rows[:].rearrange("p j k -> p (j k)"), op=ALU.mult)
            held["scaled", q, l, h] = scaled

        def turn_x(q, l, h):
            words = held["scaled", q, l, h][:].bitcast(F32)
            bank, index = take_bank()
            for j in range(2):
                for u in range(2):
                    nc.tensor.transpose(bank[:, (2 * j + u) * P:(2 * j + u + 1) * P],
                                        words[:, j * 2 * P + u:(j + 1) * 2 * P:2], ident[:])
            held["x_bank", q, l, h] = (bank, index)

        def empty_words(bank_key, grouped_key, h):
            if h == 0:
                held[grouped_key] = interleaved_tile()
            bank, index = held[bank_key]
            words = held[grouped_key][:].bitcast(F32)[:, h * T:(h + 1) * T]
            nc.scalar.copy(out=words.rearrange("p (j r u) -> p j r u", j=2, u=2),
                           in_=bank[:].rearrange("p (j u r) -> p j r u", j=2, u=2))
            free_banks.append(index)

        def empty_x(q, l, h):
            empty_words(("x_bank", q, l, h), ("x_grouped", q, l), h)

        def quantise_x(q, l):
            if l == MIDDLE:
                held["x", q, l] = quantise(held["x_grouped", q, l], "x_middle", GROUP_MAX + 2)
            else:
                held["x", q, l] = quantise(held["x_grouped", q, l], "x_neighbour", 2)

        def multiply_neighbour(q, n, c):
            held["e_bank", q, n, c] = product(held["weights", "we_paired"], c, held["x", q, NEIGHBOUR_OF[n]])

        def empty_neighbour(q, n, c):
            if c == 0:
                held["n_tags", q, n] = new_tile("n_tags", [P, CHUNKS, QUAD], F32, 3)
            bank, index = held["e_bank", q, n, c]
            nc.scalar.activation(out=held["n_tags", q, n][:, c, :], in_=bank[:], func=ACT.Identity, bias=bias_cols[:, c, n:n + 1])
            free_banks.append(index)

        def turn_upper_halves(q, n, h):
            bank, index = take_bank(BF16, 2 * T)
            for i in range(2):
                j = 2 * h + i
                for c in range(CHUNKS):
                    halves = held["n_tags", q, n][:, c, :].bitcast(BF16)
                    nc.tensor.transpose(bank[:, i * T + c * P:i * T + (c + 1) * P],
                                        halves[:, 2 * j * P + 1:2 * (j + 1) * P:2], ident_half[:])
            held["top_bank", q, n, h] = (bank, index)

        def neighbour_max(q, n, j):
            if j == 0:
                held["neg_max", q, n] = new_tile("neg_max", [P, TILES], F32, 3)
            bank, index = held["top_bank", q, n, j // 2]
            negated = new_tile("negated", [P, T], BF16, 2)
            nc.vector.tensor_scalar(out=negated[:], in0=bank[:, (j % 2) * T:(j % 2 + 1) * T], scalar1=-1.0, scalar2=None,
                                    op0=ALU.mult, op1=ALU.min, accum_out=held["neg_max", q, n][:, j:j + 1])
            if j % 2 == 1:
                free_banks.append(index)

        def turn_neighbour(q, n, j):
            bank, index = take_bank()
            for c in range(CHUNKS):
                nc.tensor.transpose(bank[:, c * P:(c + 1) * P], held["n_tags", q, n][:, c, j * P:(j + 1) * P], ident[:])
            held["n_bank", q, n, j] = (bank, index)

        def neighbour_exp(q, n, j):
            if j == 0:
                held["sums", q, n] = new_tile("sums", [P, TILES], F32, 3)
            bank, index = held["n_bank", q, n, j]
            exps = exp_tile()
            nc.scalar.activation(out=exps[:], in_=bank[:], func=ACT.Exp, bias=held["neg_max", q, n][:, j:j + 1],
                                 accum_out=held["sums", q, n][:, j:j + 1])
            free_banks.append(index)
            held["exps", q, n, j] = exps

        def reciprocals(q, n, h):
            if h == 0:
                held["recip", q, n] = new_tile("recip", [P, TILES], F32, 3)
            nc.vector.reciprocal(out=held["recip", q, n][:, 2 * h:2 * h + 2], in_=held["sums", q, n][:, 2 * h:2 * h + 2])

        def apply_gain(q, n, j):
            if j % 2 == 0:
                held["v", q, n, j // 2] = new_tile("v", [P, 2, T], BF16, 2)
            nc.vector.scalar_tensor_tensor(
                out=held["v", q, n, j // 2][:, j % 2, :], in0=held["exps", q, n, j][:], scalar=held["recip", q, n][:, j:j + 1],
                in1=gain_rows[:, n, :], op0=ALU.mult, op1=ALU.mult)

        def turn_v(q, n, h):
            words = held["v", q, n, h][:].rearrange("p j t -> p (j t)").bitcast(F32)
            bank, index = take_bank()
            for i in range(2 * 2):
                nc.tensor.transpose(bank[:, i * P:(i + 1) * P], words[:, i * P:(i + 1) * P], ident[:])
            held["v_bank", q, n, h] = (bank, index)

        def empty_v(q, n, h):
            empty_words(("v_bank", q, n, h), ("v_grouped", q, n), h)

        def quantise_v(q, n):
            held["v_codes", q, n] = quantise(held["v_grouped", q, n], "v", NB * GROUP_MAX + 1)

        def multiply_message(q, n, c):
            held["m_bank", q, n, c] = product(held["weights", ("trans", n)], c, held["v_codes", q, n])

        def floor_message(q, n, c):
            bank, index = held["m_bank", q, n, c]
            if n == 0:
                held["floored", q, c] = new_tile("floored", [P, NB, QUAD], F32, LOG_LAG + EARLY // 2)
                nc.vector.tensor_scalar(out=held["floored", q, c][:, n, :], in0=bank[:], scalar1=KNEE, scalar2=0.0,
                                        op0=ALU.add, op1=ALU.max)
            else:
                nc.scalar.activation(out=held["floored", q, c][:, n, :], in_=bank[:], func=ACT.Relu, bias=knee[:])
            free_banks.append(index)

        def log_messages(q, c):
            logs = new_tile("logs", [P, NB, QUAD], F32, 2 * CHUNKS + 1)
            nc.scalar.activation(out=logs[:], in_=held["floored", q, c][:], func=ACT.Ln, scale=SLOPE, bias=one[:])
            held["logs", q, c] = logs

        def multiply_middle(q, c):
            held["middle_bank", q, c] = product(held["weights", "we_plain"], c, held["x", q, MIDDLE])

        def add_middle(q, c):
            bank, index = held["middle_bank", q, c]
            first_log = held["logs", q, c][:, 0, :]
            nc.vector.scalar_tensor_tensor(out=first_log, in0=bank[:], scalar=bias_cols[:, c, BE_ROW:BE_ROW + 1], in1=first_log,
                                           op0=ALU.add, op1=ALU.add)
            free_banks.append(index)

        def turn_scores(q, j):
            bank, index = take_bank()
            for c in range(CHUNKS):
                for n in range(NB):
                    nc.tensor.matmul(bank[:, c * P:(c + 1) * P], lhsT=held["logs", q, c][:, n, j * P:(j + 1) * P], rhs=ident[:],
                                     start=(n == 0), stop=(n == NB - 1), is_transpose=True)
            held["score_bank", q, j] = (bank, index)

        def empty_scores(q, j):
            if j == 0:
                held["neg_scores", q] = score_tile()
                held["neg_top", q] = new_tile("neg_top", [P, TILES], F32, QUADS)
            bank, index = held["score_bank", q, j]
            nc.vector.tensor_scalar(out=held["neg_scores", q][:, j, :], in0=bank[:], scalar1=-1.0, scalar2=None,
                                    op0=ALU.mult, op1=ALU.min, accum_out=held["neg_top", q][:, j:j + 1])
            free_banks.append(index)

        def score_exp(q, j):
            if j == 0:
                held["total", q] = new_tile("total", [P, TILES], F32, QUADS)
            terms = new_tile("terms", [P, T], BF16, 2)
            nc.scalar.activation(out=terms[:], in_=held["neg_scores", q][:, j, :], func=ACT.Exp, scale=-1.0,
                                 bias=held["neg_top", q][:, j:j + 1], accum_out=held["total", q][:, j:j + 1])

        def log_total(q):
            log_mean = new_tile("log_mean", [P, TILES], F32, QUADS)
            nc.scalar.activation(out=log_mean[:], in_=held["total", q][:], func=ACT.Ln, scale=1.0 / T)
            held["log_mean", q] = log_mean

        def make_shift(q):
            shift = new_tile("shift", [P, TILES], F32, QUADS)
            nc.vector.tensor_tensor(out=shift[:], in0=held["neg_top", q][:], in1=held["log_mean", q][:], op=ALU.subtract)
            held["shift", q] = shift

        def finish(q, j, engine):
            row = held["neg_scores", q][:, j, :]
            engine.tensor_scalar(out=row, in0=row, scalar1=-1.0, scalar2=held["shift", q][:, j:j + 1], op0=ALU.mult, op1=ALU.add)
            rows = out[q * QUAD:(q + 1) * QUAD, :].rearrange("(r j) t -> r j t", j=TILES)
            nc.sync.dma_start(out=rows[:, j, :], in_=row)

        events = []

        def at(step, place, call, *args):
            events.append((step, place, len(events), call, args))

        def plan_x(q, due):
            for l, offsets in SCALE_STEPS:
                if q > 0:
                    at(due + offsets[0] - LOAD_LEAD, 0, load_bytes, q, l)
                for h in range(2):
                    at(due + offsets[h], 3, scale_x, q, l, h)
                    at(due + offsets[h] + 1, 8, turn_x, q, l, h)
                    at(due + offsets[h] + 2, 7, empty_x, q, l, h)
                at(due + offsets[1] + 3, 11, quantise_x, q, l)
            for n in range(NB):
                for c in range(CHUNKS):
                    step = due + EMPTY_FIRST + n * CHUNKS + c
                    at(step - 1 - c % 2, 12, multiply_neighbour, q, n, c)
                    at(step, 4, empty_neighbour, q, n, c)

        def plan_messages(q, base):
            for n in range(NB):
                for j in range(TILES):
                    step = base + n * TILES + j
                    at(step - 1, 2, turn_neighbour, q, n, j)
                    if j % 2 == 0:
                        at(step - 2, 12, turn_upper_halves, q, n, j // 2)
                    at(step - 1 - j % 2, 6, neighbour_max, q, n, j)
                    at(step, 1, neighbour_exp, q, n, j)
                    at(step + GAIN_LAG, 9, apply_gain, q, n, j)
                    if j % 2 == 1:
                        at(step + 1, 10, reciprocals, q, n, j // 2)
                        at(step + GAIN_LAG + 1, 5, turn_v, q, n, j // 2)
                        at(step + GAIN_LAG + 1, 10, empty_v, q, n, j // 2)
                at(base + (n + 1) * TILES + GAIN_LAG + 1, 11, quantise_v, q, n)

        def plan_logs(q, base, group_base):
            for c in range(CHUNKS):
                step = base + c
                early = max(0, EARLY - (step - group_base))
                for n in range(NB):
                    at(step - early, 5, multiply_message, q, n, c)
                    at(step - early + 1, 3 + n, floor_message, q, n, c)
                at(step + LOG_LAG, 1, log_messages, q, c)
                at(step + LOG_LAG, 5, multiply_middle, q, c)
                at(step + LOG_LAG + 1, 4, add_middle, q, c)
            for j in range(TILES):
                at(base + CHUNKS + LOG_LAG + 1 + j, 0, turn_scores, q, j)
                at(base + CHUNKS + LOG_LAG + 1 + j, 8, empty_scores, q, j)

        def plan_score_exps(quads, base, steps):
            rows = [(q, j) for q in quads for j in range(TILES)]
            for i, (q, j) in enumerate(rows):
                at(base + i * steps // len(rows), 13, score_exp, q, j)

        def plan_finish(quads, base, gap, engine):
            for i, q in enumerate(quads):
                at(base + i * gap, 0, log_total, q)
                at(base + i * gap + 1, 0, make_shift, q)
                for j in range(TILES):
                    at(base + i * gap + 1, 9, finish, q, j, engine)

        head = SCALE_STEPS[0][1][0] - LOAD_LEAD
        first_copy = SCALE_STEPS[0][1][0] + 2
        at(head, 0, load_first)
        at(head, 1, make_constants)
        at(head, 2, make_scales)
        at(first_copy, 5, interleave_we_paired)
        at(first_copy + 1, 5, make_biases)
        at(first_copy + 1, 11, quantise_weights, "we_paired")
        at(first_copy + 1, 13, interleave_we_plain)
        at(first_copy + 4, 13, quantise_weights, "we_plain")
        for n in range(NB):
            at(first_copy + 3 * (n + 1), 13, interleave_trans, n)
            at(first_copy + 3 * (n + 2), 13, quantise_weights, ("trans", n))
            at(n - NB, 13, make_gains, n)

        plan_x(0, 0)
        step = 0
        previous = []
        for g, size in enumerate(GROUPS):
            quads = list(range(sum(GROUPS[0:g]), sum(GROUPS[0:g + 1])))
            if previous:
                plan_score_exps(previous, step + 1, size * EXP_STEPS - 1)
            for q in quads:
                plan_messages(q, step)
                step = step + EXP_STEPS
                if q + 1 < QUADS:
                    plan_x(q + 1, step + (X_DELAY if q == quads[-1] else 0))
            if previous:
                plan_finish(previous, step + FINISH_GAP, FINISH_GAP, nc.gpsimd)
            step = max(step - LOG_LAG, step + GAIN_LAG + 2 - (size - 1) * CHUNKS)
            group_base = step
            for q in quads:
                plan_logs(q, step, group_base)
                step = step + CHUNKS
            step = step + LOG_LAG
            previous = quads
        plan_score_exps(previous, step + 1, len(previous) * TILES)
        plan_finish(previous, step + 1 + len(previous) * TILES, 0, nc.vector)

        for event in sorted(events, key=lambda entry: entry[0:3]):
            event[3](*event[4])
